import numpy as np
import ml_dtypes

BF16 = ml_dtypes.bfloat16


def bf(x):
    return np.asarray(x, np.float32).astype(BF16)


def f32(x):
    return np.asarray(x, np.float32)


def f64(x):
    return np.asarray(x).astype(np.float64)


def striped(idx):
    return np.tile(idx.reshape(-1, 16).T, (8, 1))


S, K, M, N, D, V = 1024, 256, 256, 2048, 8, 256


def sigmoid(v):
    return 1.0 / (1.0 + np.exp(-v))


def setup_inputs():
    return {"table": bf(np.random.standard_normal((K, S))), "w": bf(np.random.standard_normal((K, M)) / np.sqrt(K)), "b": f32(0.5 * np.random.standard_normal((M, 1))), "offs": striped(np.random.permutation(np.tile(np.arange(S), 2))[:N])}


def reference(table, w, b, offs):
    idx = offs[:16].T.reshape(-1)
    x = f64(table)[:, idx]
    y = f64(w).T @ x
    z = (y + f64(b)) * sigmoid(y + f64(b))
    return z.reshape(M, V, D).mean(axis=2)

@@ -1,0 +1,67 @@
+import concourse.mybir as mybir
+
+F32, BF16, U16 = mybir.dt.float32, mybir.dt.bfloat16, mybir.dt.uint16
+SILU = mybir.ActivationFunctionType.Silu
+ADD = mybir.AluOpType.add
+
+P = 128
+K, M, S = 256, 256, 1024
+N, D = 2048, 8
+V = N // D
+PIECE = 512
+K_BLOCKS, M_BLOCKS, PIECES = K // P, M // P, N // PIECE
+PIECE_V = PIECE // D
+FLOPS = 2 * K * M * N
+
+
+def tile_gather_matmul_kernel(tc, table, w, b, offs, out):
+    nc = tc.nc
+    with (
+        tc.tile_pool(name="held", bufs=1) as held,
+        tc.tile_pool(name="work", bufs=3) as work,
+        tc.psum_pool(name="psum", bufs=M_BLOCKS * PIECES) as psum,
+    ):
+        offsets = held.tile([P, N // 16], U16)
+        nc.sync.dma_start(offsets[:], offs)
+
+        weights = held.tile([P, K_BLOCKS, M], BF16)
+        nc.scalar.dma_start(weights[:], w.rearrange("(kb p) m -> p kb m", p=P))
+
+        blocks = []
+        for kb in range(K_BLOCKS):
+            block = held.tile([P, S], BF16, name=f"block{kb}")
+            nc.sync.dma_start(block[:], table[kb * P : (kb + 1) * P, :])
+            blocks.append(block)
+
+        bias = held.tile([P, M_BLOCKS], F32)
+        nc.scalar.dma_start(bias[:], b.rearrange("(mb p) o -> p (mb o)", p=P))
+
+        warm = held.tile([P, 1], F32)
+        nc.vector.memset(warm[:], 0.0)
+        warm_out = held.tile([P, 1], F32)
+        nc.scalar.activation(warm_out[:], warm[:], SILU)
+
+        for mb in range(M_BLOCKS):
+            sums = held.tile([P, V], F32, name=f"sums{mb}")
+            for piece in range(PIECES):
+                bank = psum.tile([P, PIECE], F32)
+                for kb in range(K_BLOCKS):
+                    picked = offsets[:, piece * (PIECE // 16) : (piece + 1) * (PIECE // 16)]
+                    nc.tensor.matmul(
+                        bank[:],
+                        weights[:, kb, mb * P : (mb + 1) * P],
+                        blocks[kb][:].indirect(picked),
+                        start=(kb == 0),
+                        stop=(kb == K_BLOCKS - 1),
+                    )
+                z = work.tile([P, PIECE], F32)
+                nc.scalar.activation(z[:], bank[:], SILU, bias=bias[:, mb : mb + 1])
+                nc.vector.tensor_reduce(
+                    sums[:, piece * PIECE_V : (piece + 1) * PIECE_V],
+                    z[:].rearrange("p (v t) -> p v t", t=D),
+                    axis=mybir.AxisListType.X,
+                    op=ADD,
+                )
+            means = held.tile([P, V], F32, name=f"means{mb}")
+            nc.vector.tensor_scalar_mul(means[:], sums[:], 1.0 / D)
+            nc.sync.dma_start(out[mb * P : (mb + 1) * P, :], means[:])

@@ -11,6 +11,7 @@ V = N // D
 PIECE = 512
 K_BLOCKS, M_BLOCKS, PIECES = K // P, M // P, N // PIECE
 PIECE_V = PIECE // D
+HALF = PIECE // 2
 FLOPS = 2 * K * M * N
 
 
@@ -18,7 +19,7 @@ def tile_gather_matmul_kernel(tc, table, w, b, offs, out):
     nc = tc.nc
     with (
         tc.tile_pool(name="held", bufs=1) as held,
-        tc.tile_pool(name="work", bufs=3) as work,
+        tc.tile_pool(name="work", bufs=4) as work,
         tc.psum_pool(name="psum", bufs=M_BLOCKS * PIECES) as psum,
     ):
         offsets = held.tile([P, N // 16], U16)
@@ -34,7 +35,7 @@ def tile_gather_matmul_kernel(tc, table, w, b, offs, out):
             blocks.append(block)
 
         bias = held.tile([P, M_BLOCKS], F32)
-        nc.scalar.dma_start(bias[:], b.rearrange("(mb p) o -> p (mb o)", p=P))
+        nc.sync.dma_start(bias[:], b.rearrange("(mb p) o -> p (mb o)", p=P))
 
         warm = held.tile([P, 1], F32)
         nc.vector.memset(warm[:], 0.0)
@@ -42,7 +43,6 @@ def tile_gather_matmul_kernel(tc, table, w, b, offs, out):
         nc.scalar.activation(warm_out[:], warm[:], SILU)
 
         for mb in range(M_BLOCKS):
-            sums = held.tile([P, V], F32, name=f"sums{mb}")
             for piece in range(PIECES):
                 bank = psum.tile([P, PIECE], F32)
                 for kb in range(K_BLOCKS):
@@ -54,14 +54,20 @@ def tile_gather_matmul_kernel(tc, table, w, b, offs, out):
                         start=(kb == 0),
                         stop=(kb == K_BLOCKS - 1),
                     )
-                z = work.tile([P, PIECE], F32)
-                nc.scalar.activation(z[:], bank[:], SILU, bias=bias[:, mb : mb + 1])
-                nc.vector.tensor_reduce(
-                    sums[:, piece * PIECE_V : (piece + 1) * PIECE_V],
-                    z[:].rearrange("p (v t) -> p v t", t=D),
-                    axis=mybir.AxisListType.X,
-                    op=ADD,
+                sums = work.tile([P, PIECE_V], F32)
+                for half in range(2):
+                    z = work.tile([P, HALF], F32)
+                    nc.scalar.activation(
+                        z[:], bank[:, half * HALF : (half + 1) * HALF], SILU, bias=bias[:, mb : mb + 1]
+                    )
+                    nc.vector.tensor_reduce(
+                        sums[:, half * (HALF // D) : (half + 1) * (HALF // D)],
+                        z[:].rearrange("p (v t) -> p v t", t=D),
+                        axis=mybir.AxisListType.X,
+                        op=ADD,
+                    )
+                means = work.tile([P, PIECE_V], F32)
+                nc.vector.tensor_scalar_mul(means[:], sums[:], 1.0 / D)
+                nc.sync.dma_start(
+                    out[mb * P : (mb + 1) * P, piece * PIECE_V : (piece + 1) * PIECE_V], means[:]
                 )
-            means = held.tile([P, V], F32, name=f"means{mb}")
-            nc.vector.tensor_scalar_mul(means[:], sums[:], 1.0 / D)
-            nc.sync.dma_start(out[mb * P : (mb + 1) * P, :], means[:])

@@ -26,12 +26,12 @@ def tile_gather_matmul_kernel(tc, table, w, b, offs, out):
         nc.sync.dma_start(offsets[:], offs)
 
         weights = held.tile([P, K_BLOCKS, M], BF16)
-        nc.scalar.dma_start(weights[:], w.rearrange("(kb p) m -> p kb m", p=P))
+        nc.sync.dma_start(weights[:], w.rearrange("(kb p) m -> p kb m", p=P))
 
         blocks = []
         for kb in range(K_BLOCKS):
             block = held.tile([P, S], BF16, name=f"block{kb}")
-            nc.sync.dma_start(block[:], table[kb * P : (kb + 1) * P, :])
+            (nc.scalar if kb == 0 else nc.sync).dma_start(block[:], table[kb * P : (kb + 1) * P, :])
             blocks.append(block)
 
         bias = held.tile([P, M_BLOCKS], F32)
@@ -43,6 +43,7 @@ def tile_gather_matmul_kernel(tc, table, w, b, offs, out):
         nc.scalar.activation(warm_out[:], warm[:], SILU)
 
         for mb in range(M_BLOCKS):
+            means = held.tile([P, V], F32, name=f"means{mb}")
             for piece in range(PIECES):
                 bank = psum.tile([P, PIECE], F32)
                 for kb in range(K_BLOCKS):
@@ -66,8 +67,5 @@ def tile_gather_matmul_kernel(tc, table, w, b, offs, out):
                         axis=mybir.AxisListType.X,
                         op=ADD,
                     )
-                means = work.tile([P, PIECE_V], F32)
-                nc.vector.tensor_scalar_mul(means[:], sums[:], 1.0 / D)
-                nc.sync.dma_start(
-                    out[mb * P : (mb + 1) * P, piece * PIECE_V : (piece + 1) * PIECE_V], means[:]
-                )
+                nc.vector.tensor_scalar_mul(means[:, piece * PIECE_V : (piece + 1) * PIECE_V], sums[:], 1.0 / D)
+            nc.sync.dma_start(out[mb * P : (mb + 1) * P, :], means[:])

import concourse.mybir as mybir

F32, BF16, U16 = mybir.dt.float32, mybir.dt.bfloat16, mybir.dt.uint16
SILU = mybir.ActivationFunctionType.Silu
ADD = mybir.AluOpType.add

P = 128
K, M, S = 256, 256, 1024
N, D = 2048, 8
V = N // D
PIECE = 512
K_BLOCKS, M_BLOCKS, PIECES = K // P, M // P, N // PIECE
PIECE_V = PIECE // D
HALF = PIECE // 2
FLOPS = 2 * K * M * N


def tile_gather_matmul_kernel(tc, table, w, b, offs, out):
    nc = tc.nc
    with (
        tc.tile_pool(name="held", bufs=1) as held,
        tc.tile_pool(name="work", bufs=4) as work,
        tc.psum_pool(name="psum", bufs=M_BLOCKS * PIECES) as psum,
    ):
        offsets = held.tile([P, N // 16], U16)
        nc.sync.dma_start(offsets[:], offs)

        weights = held.tile([P, K_BLOCKS, M], BF16)
        nc.sync.dma_start(weights[:], w.rearrange("(kb p) m -> p kb m", p=P))

        blocks = []
        for kb in range(K_BLOCKS):
            block = held.tile([P, S], BF16, name=f"block{kb}")
            (nc.scalar if kb == 0 else nc.sync).dma_start(block[:], table[kb * P : (kb + 1) * P, :])
            blocks.append(block)

        bias = held.tile([P, M_BLOCKS], F32)
        nc.sync.dma_start(bias[:], b.rearrange("(mb p) o -> p (mb o)", p=P))

        warm = held.tile([P, 1], F32)
        nc.vector.memset(warm[:], 0.0)
        warm_out = held.tile([P, 1], F32)
        nc.scalar.activation(warm_out[:], warm[:], SILU)

        for mb in range(M_BLOCKS):
            means = held.tile([P, V], F32, name=f"means{mb}")
            for piece in range(PIECES):
                bank = psum.tile([P, PIECE], F32)
                for kb in range(K_BLOCKS):
                    picked = offsets[:, piece * (PIECE // 16) : (piece + 1) * (PIECE // 16)]
                    nc.tensor.matmul(
                        bank[:],
                        weights[:, kb, mb * P : (mb + 1) * P],
                        blocks[kb][:].indirect(picked),
                        start=(kb == 0),
                        stop=(kb == K_BLOCKS - 1),
                    )
                sums = work.tile([P, PIECE_V], F32)
                for half in range(2):
                    z = work.tile([P, HALF], F32)
                    nc.scalar.activation(
                        z[:], bank[:, half * HALF : (half + 1) * HALF], SILU, bias=bias[:, mb : mb + 1]
                    )
                    nc.vector.tensor_reduce(
                        sums[:, half * (HALF // D) : (half + 1) * (HALF // D)],
                        z[:].rearrange("p (v t) -> p v t", t=D),
                        axis=mybir.AxisListType.X,
                        op=ADD,
                    )
                nc.vector.tensor_scalar_mul(means[:, piece * PIECE_V : (piece + 1) * PIECE_V], sums[:], 1.0 / D)
            nc.sync.dma_start(out[mb * P : (mb + 1) * P, :], means[:])
